import numpy as np
import ml_dtypes


def mxq(x, axis, fmt="e4m3"):
    dtype, down = {"e4m3": (ml_dtypes.float8_e4m3fn, 7), "e5m2": (ml_dtypes.float8_e5m2, 14)}[fmt]
    v = np.moveaxis(np.asarray(x, np.float32).astype(ml_dtypes.bfloat16).astype(np.float64), axis, -1)
    blocks = v.reshape(v.shape[:-1] + (-1, 32))
    amax = np.abs(blocks).max(-1, keepdims=True)
    byte = np.maximum(np.where(amax > 0, np.frexp(amax)[1] - 1 + 127, 0) - down, 1)
    scale = np.exp2(byte - 127.0)
    codes = (blocks / scale).astype(np.float32).astype(dtype).astype(np.float64)
    return np.moveaxis((codes * scale).reshape(v.shape), -1, axis)


WIDE = False


def mx_kscale(k):
    if not WIDE:
        return np.ones(k)
    levels = np.array([10, -10, 5, -5, 0])
    if k % 512:
        return np.exp2(np.random.permutation(np.resize(levels, k // 32))).repeat(32)
    a = np.empty((k // 512, 16))
    for p in range(k // 512):
        a[p, :8] = np.random.permutation(np.resize(levels, 8))
        for g in range(8):
            far = levels[np.abs(levels - a[p, g]) >= 10]
            a[p, g + 8] = far[np.random.randint(len(far))]
    return np.exp2(a.ravel()).repeat(32)


def f64(x):
    return np.asarray(x).astype(np.float64)


def split(x):
    m, e = np.frexp(f64(x))
    hi = np.ldexp(np.trunc(16.0 * m) / 16.0, e)
    return hi, f64(x) - hi


K, M, T = 1024, 512, 512


def setup_inputs():
    n = np.random.standard_normal
    s = mx_kscale(K)[:, None]
    return {
        "w": (n((K, M)) / np.sqrt(K) / s).astype(np.float32),
        "x": (n((K, T)) * s).astype(np.float32),
        "r": (n((512, 512))).astype(np.float32),
    }


def reference(w, x, r):
    w_hi, w_lo = split(w)
    w_hi_, w_lo_ = mxq(w_hi, 0, "e4m3"), mxq(w_lo, 0, "e4m3")
    x_hi, x_lo = split(x)
    x_hi_, x_lo_ = mxq(x_hi, 0, "e4m3"), mxq(x_lo, 0, "e4m3")
    y = w_hi_.T @ x_hi_ + w_hi_.T @ x_lo_ + w_lo_.T @ x_hi_
    return f64(r) + y

@@ -1,0 +1,203 @@
+from contextlib import ExitStack
+
+import concourse.mybir as mybir
+
+K, N, T = 1024, 512, 512
+FLOPS = 3 * 2 * K * N * T
+
+F32 = mybir.dt.float32
+BF16 = mybir.dt.bfloat16
+I32 = mybir.dt.int32
+U32 = mybir.dt.uint32
+U8 = mybir.dt.uint8
+FP8X4 = mybir.dt.float8_e4m3fn_x4
+AND = mybir.AluOpType.bitwise_and
+SUB = mybir.AluOpType.subtract
+ADD = mybir.AluOpType.add
+
+P = 128
+PACK = 4
+K_PASS = P * PACK
+MASK_ONE = -1048576
+MASK_TWO = -983056
+
+
+def tile_mix_split3_fm_res_kernel(tc, w, x, r, out):
+    nc = tc.nc
+    with ExitStack() as ctx:
+        pool = ctx.enter_context(tc.tile_pool(name="pool", bufs=1))
+        psum = ctx.enter_context(tc.psum_pool(name="psum", bufs=1))
+        ctx.enter_context(tc.manual_schedule())
+
+        def sb(shape, dtype, name):
+            t = pool.tile(shape, dtype, name=name, tag=name, align_bytes=64)
+            return t
+
+        def load(src, g, c0, c1, name):
+            t = sb([P, PACK, c1 - c0], F32, name)
+            nc.sync.dma_start(out=t[:], in_=src[g * K_PASS : (g + 1) * K_PASS, c0:c1].rearrange("(p j) w -> p j w", j=PACK))
+            return t
+
+        x0 = [load(x, 0, c, c + 128, "x0_" + str(c)) for c in range(0, 512, 128)]
+        x1 = [load(x, 1, c, c + 256, "x1_" + str(c)) for c in range(0, 512, 256)]
+        wr = {}
+        for h in (0, 1):
+            for g in (0, 1):
+                wr[g, h] = load(w, g, 256 * h, 256 * h + 256, "w" + str(g) + str(h))
+        r_sb = sb([P, 4, T], F32, "r_sb")
+        nc.sync.dma_start(out=r_sb[:], in_=r.rearrange("(m p) t -> p m t", p=P))
+
+        xq = {(g, part): sb([P, T], U32, "xq" + str(g) + part) for g in (0, 1) for part in ("hi", "lo")}
+        xs = {(g, part): sb([P, T], U8, "xs" + str(g) + part) for g in (0, 1) for part in ("hi", "lo")}
+
+        def rows(ap):
+            return ap.rearrange("p j (c i) -> p c j i", i=4)
+
+        def packed(ap):
+            return ap.rearrange("p (c i j) -> p c j i", i=4, j=PACK)
+
+        def unit(name, pieces, full):
+            n = sum(p[2] for p in pieces) * PACK
+            offs = [sum(p[2] for p in pieces[:i]) * PACK for i in range(len(pieces))]
+            return dict(name=name, pieces=pieces, n=n, offs=offs,
+                        top=None if full else sb([P, n], BF16, "top_" + name),
+                        hi32=sb([P, PACK, n // PACK], I32, "hi32_" + name) if full else None,
+                        hl=sb([P, 2 * n], BF16, "hl_" + name))
+
+        def trunc32(u, a, b):
+            raw, r0, width = u["pieces"][0]
+            nc.vector.tensor_scalar(out=u["hi32"][:, :, a:b], in0=raw[:, :, r0 + a : r0 + b].bitcast(I32), scalar1=MASK_ONE, scalar2=None, op0=AND)
+
+        def cast_hi(u):
+            nc.scalar.copy(out=packed(u["hl"][:, 0 : u["n"]]), in_=rows(u["hi32"][:].bitcast(F32)))
+
+        def top_copy(u):
+            for (raw, r0, width), o in zip(u["pieces"], u["offs"]):
+                s = raw[:].bitcast(BF16)[:, :, 2 * r0 + 1 : 2 * (r0 + width) : 2]
+                nc.scalar.copy(out=packed(u["top"][:, o : o + width * PACK]), in_=rows(s))
+
+        def trunc(u):
+            nc.vector.tensor_scalar(out=u["hl"][:, 0 : u["n"]].bitcast(I32), in0=u["top"][:].bitcast(I32), scalar1=MASK_TWO, scalar2=None, op0=AND)
+
+        def sub(u, i=0, a=0, b=None):
+            raw, r0, width = u["pieces"][i]
+            b = width if b is None else b
+            o = u["offs"][i]
+            if u["hi32"] is not None:
+                in1 = rows(u["hi32"][:, :, a:b].bitcast(F32))
+            else:
+                in1 = packed(u["hl"][:, o + 4 * a : o + 4 * b])
+            nc.vector.tensor_tensor(out=packed(u["hl"][:, u["n"] + o + 4 * a : u["n"] + o + 4 * b]), in0=rows(raw[:, :, r0 + a : r0 + b]), in1=in1, op=SUB)
+
+        def quant_x(u, g, c0, part):
+            n = u["n"]
+            s = slice(c0, c0 + n // 4)
+            src = u["hl"][:, 0:n] if part == "hi" else u["hl"][:, n : 2 * n]
+            nc.vector.quantize_mx(out=xq[g, part][:, s].bitcast(FP8X4), scales=xs[g, part][:, s], in_=src)
+
+        wcodes = {}
+
+        def w_unit(name, keys):
+            u = unit(name, [(wr[g, m // 2], 128 * (m % 2), 128) for (g, m) in keys], False)
+            u["codes"] = sb([P, u["n"] // 2], U32, "wq_" + name)
+            u["scales"] = sb([P, u["n"] // 2], U8, "ws_" + name)
+            for i, (g, m) in enumerate(keys):
+                wcodes[g, m, "hi"] = (u, 128 * i)
+                wcodes[g, m, "lo"] = (u, u["n"] // 4 + 128 * i)
+            return u
+
+        def quant_w(u, a=0, b=2):
+            h = u["n"] // 4
+            s = slice(a * h, b * h)
+            nc.vector.quantize_mx(out=u["codes"][:, s].bitcast(FP8X4), scales=u["scales"][:, s], in_=u["hl"][:, a * u["n"] : b * u["n"]])
+
+        acc = [psum.tile([P, T], F32, name="acc" + str(m)) for m in range(4)]
+
+        def product(m, g, wpart, xpart, start, stop):
+            u, c = wcodes[g, m, wpart]
+            s = slice(c, c + P)
+            nc.tensor.matmul_mx(out=acc[m][:], lhsT=u["codes"][:, s].bitcast(FP8X4), lhsT_scale=u["scales"][:, s],
+                                rhs=xq[g, xpart][:].bitcast(FP8X4), rhs_scale=xs[g, xpart][:], start=start, stop=stop)
+
+        def products(m, g):
+            product(m, g, "hi", "hi", g == 0, False)
+            product(m, g, "hi", "lo", False, False)
+            product(m, g, "lo", "hi", False, g == 1)
+
+        y = [sb([P, T], F32, "y" + str(m)) for m in range(4)]
+
+        def drain(m, a, b):
+            nc.vector.tensor_tensor(out=y[m][:, a:b], in0=acc[m][:, a:b], in1=r_sb[:, m, a:b], op=ADD)
+            nc.sync.dma_start(out=out[m * P : (m + 1) * P, a:b], in_=y[m][:, a:b])
+
+        xa, xb, xc = [unit("xa" + str(i), [(x0[i], 0, 128)], True) for i in range(3)]
+        xd = unit("xd", [(x0[3], 0, 128)], False)
+        xe, xf = [unit("xe" + str(i), [(x1[i], 0, 256)], False) for i in range(2)]
+        p0 = w_unit("p0", [(0, 0), (1, 0)])
+        p1 = w_unit("p1", [(0, 1), (1, 1)])
+        p2 = w_unit("p2", [(0, 2), (0, 3)])
+        u6 = w_unit("u6", [(1, 2)])
+        u7 = w_unit("u7", [(1, 3)])
+
+        trunc32(xa, 0, 64)
+        trunc32(xa, 64, 128)
+        cast_hi(xa)
+        sub(xa, 0, 0, 64)
+        sub(xa, 0, 64, 128)
+        trunc32(xb, 0, 128)
+        cast_hi(xb)
+        top_copy(xd)
+        quant_x(xa, 0, 0, "lo")
+        sub(xb)
+        quant_x(xa, 0, 0, "hi")
+        trunc32(xc, 0, 128)
+        cast_hi(xc)
+        quant_x(xb, 0, 128, "lo")
+        sub(xc)
+        quant_x(xb, 0, 128, "hi")
+        for u, prev in ((xd, (xc, 0, 256)), (xe, (xd, 0, 384)), (xf, (xe, 1, 0))):
+            if u is not xd:
+                top_copy(u)
+            trunc(u)
+            quant_x(*prev, "lo")
+            sub(u)
+            quant_x(*prev, "hi")
+        top_copy(p0)
+        trunc(p0)
+        quant_x(xf, 1, 256, "lo")
+        sub(p0, 0)
+        quant_x(xf, 1, 256, "hi")
+        sub(p0, 1)
+        top_copy(p1)
+        trunc(p1)
+        quant_w(p0)
+        products(0, 0)
+        products(0, 1)
+        sub(p1, 0)
+        sub(p1, 1)
+        top_copy(p2)
+        trunc(p2)
+        quant_w(p1)
+        products(1, 0)
+        products(1, 1)
+        sub(p2, 0)
+        sub(p2, 1)
+        top_copy(u6)
+        trunc(u6)
+        drain(0, 0, T)
+        quant_w(p2)
+        products(2, 0)
+        products(3, 0)
+        sub(u6)
+        top_copy(u7)
+        trunc(u7)
+        drain(1, 0, T)
+        quant_w(u6)
+        products(2, 1)
+        sub(u7)
+        quant_w(u7, 0, 1)
+        quant_w(u7, 1, 2)
+        products(3, 1)
+        drain(2, 0, T)
+        drain(3, 0, 256)
+        drain(3, 256, T)

@@ -38,7 +38,7 @@ def tile_mix_split3_fm_res_kernel(tc, w, x, r, out):
             nc.sync.dma_start(out=t[:], in_=src[g * K_PASS : (g + 1) * K_PASS, c0:c1].rearrange("(p j) w -> p j w", j=PACK))
             return t
 
-        x0 = [load(x, 0, c, c + 128, "x0_" + str(c)) for c in range(0, 512, 128)]
+        x0 = [load(x, 0, a, b, "x0_" + str(a)) for a, b in ((0, 128), (128, 256), (256, 384), (384, 512))]
         x1 = [load(x, 1, c, c + 256, "x1_" + str(c)) for c in range(0, 512, 256)]
         wr = {}
         for h in (0, 1):
@@ -106,10 +106,9 @@ def tile_mix_split3_fm_res_kernel(tc, w, x, r, out):
                 wcodes[g, m, "lo"] = (u, u["n"] // 4 + 128 * i)
             return u
 
-        def quant_w(u, a=0, b=2):
-            h = u["n"] // 4
-            s = slice(a * h, b * h)
-            nc.vector.quantize_mx(out=u["codes"][:, s].bitcast(FP8X4), scales=u["scales"][:, s], in_=u["hl"][:, a * u["n"] : b * u["n"]])
+        def quant_w(u, a=0, b=4):
+            s = slice(a * P, b * P)
+            nc.vector.quantize_mx(out=u["codes"][:, s].bitcast(FP8X4), scales=u["scales"][:, s], in_=u["hl"][:, a * P * PACK : b * P * PACK])
 
         acc = [psum.tile([P, T], F32, name="acc" + str(m)) for m in range(4)]
 
@@ -130,14 +129,13 @@ def tile_mix_split3_fm_res_kernel(tc, w, x, r, out):
             nc.vector.tensor_tensor(out=y[m][:, a:b], in0=acc[m][:, a:b], in1=r_sb[:, m, a:b], op=ADD)
             nc.sync.dma_start(out=out[m * P : (m + 1) * P, a:b], in_=y[m][:, a:b])
 
-        xa, xb, xc = [unit("xa" + str(i), [(x0[i], 0, 128)], True) for i in range(3)]
-        xd = unit("xd", [(x0[3], 0, 128)], False)
-        xe, xf = [unit("xe" + str(i), [(x1[i], 0, 256)], False) for i in range(2)]
+        xa, xb, xc = [unit("x0u" + str(i), [(x0[i], 0, 128)], True) for i in (0, 1, 2)]
+        xd = unit("x0u3", [(x0[3], 0, 128)], False)
+        xe, xf = [unit("x1u" + str(i), [(x1[i], 0, 256)], False) for i in (0, 1)]
         p0 = w_unit("p0", [(0, 0), (1, 0)])
         p1 = w_unit("p1", [(0, 1), (1, 1)])
         p2 = w_unit("p2", [(0, 2), (0, 3)])
-        u6 = w_unit("u6", [(1, 2)])
-        u7 = w_unit("u7", [(1, 3)])
+        p3 = w_unit("p3", [(1, 2), (1, 3)])
 
         trunc32(xa, 0, 64)
         trunc32(xa, 64, 128)
@@ -148,56 +146,64 @@ def tile_mix_split3_fm_res_kernel(tc, w, x, r, out):
         cast_hi(xb)
         top_copy(xd)
         quant_x(xa, 0, 0, "lo")
-        sub(xb)
         quant_x(xa, 0, 0, "hi")
+        sub(xb)
         trunc32(xc, 0, 128)
         cast_hi(xc)
         quant_x(xb, 0, 128, "lo")
-        sub(xc)
         quant_x(xb, 0, 128, "hi")
-        for u, prev in ((xd, (xc, 0, 256)), (xe, (xd, 0, 384)), (xf, (xe, 1, 0))):
-            if u is not xd:
-                top_copy(u)
-            trunc(u)
-            quant_x(*prev, "lo")
-            sub(u)
+        sub(xc)
+        prev = (xc, 0, 256)
+        for nxt in ((xd, 0, 384), (xe, 1, 0), (xf, 1, 256)):
+            if nxt[1] == 1:
+                top_copy(nxt[0])
+            trunc(nxt[0])
             quant_x(*prev, "hi")
+            quant_x(*prev, "lo")
+            sub(nxt[0])
+            prev = nxt
         top_copy(p0)
         trunc(p0)
-        quant_x(xf, 1, 256, "lo")
+        quant_x(*prev, "hi")
+        quant_x(*prev, "lo")
         sub(p0, 0)
-        quant_x(xf, 1, 256, "hi")
         sub(p0, 1)
         top_copy(p1)
         trunc(p1)
+        top_copy(p2)
         quant_w(p0)
         products(0, 0)
         products(0, 1)
         sub(p1, 0)
         sub(p1, 1)
-        top_copy(p2)
         trunc(p2)
+        top_copy(p3)
         quant_w(p1)
         products(1, 0)
         products(1, 1)
         sub(p2, 0)
+        trunc(p3)
         sub(p2, 1)
-        top_copy(u6)
-        trunc(u6)
-        drain(0, 0, T)
+        quant_w(p3, 0, 2)
+        for m in (2, 3):
+            product(m, 1, "hi", "hi", True, False)
+            product(m, 1, "hi", "lo", False, False)
         quant_w(p2)
-        products(2, 0)
-        products(3, 0)
-        sub(u6)
-        top_copy(u7)
-        trunc(u7)
-        drain(1, 0, T)
-        quant_w(u6)
-        products(2, 1)
-        sub(u7)
-        quant_w(u7, 0, 1)
-        quant_w(u7, 1, 2)
-        products(3, 1)
+        product(2, 0, "hi", "hi", False, False)
+        product(2, 0, "hi", "lo", False, False)
+        product(2, 0, "lo", "hi", False, False)
+        product(3, 0, "hi", "hi", False, False)
+        drain(0, 0, T)
+        sub(p3, 0)
+        drain(1, 0, 256)
+        quant_w(p3, 2, 3)
+        product(2, 1, "lo", "hi", False, True)
+        product(3, 0, "hi", "lo", False, False)
+        product(3, 0, "lo", "hi", False, False)
+        sub(p3, 1)
+        drain(1, 256, T)
+        quant_w(p3, 3, 4)
+        product(3, 1, "lo", "hi", False, True)
         drain(2, 0, T)
         drain(3, 0, 256)
         drain(3, 256, T)

@@ -11,15 +11,16 @@ I32 = mybir.dt.int32
 U32 = mybir.dt.uint32
 U8 = mybir.dt.uint8
 FP8X4 = mybir.dt.float8_e4m3fn_x4
-AND = mybir.AluOpType.bitwise_and
-SUB = mybir.AluOpType.subtract
-ADD = mybir.AluOpType.add
+ALU = mybir.AluOpType
 
 P = 128
 PACK = 4
 K_PASS = P * PACK
-MASK_ONE = -1048576
-MASK_TWO = -983056
+ROW_TILES = N // P
+HALF = 256
+
+MASK_F32 = -1048576
+MASK_BF16_PAIR = -983056
 
 
 def tile_mix_split3_fm_res_kernel(tc, w, x, r, out):
@@ -29,181 +30,170 @@ def tile_mix_split3_fm_res_kernel(tc, w, x, r, out):
         psum = ctx.enter_context(tc.psum_pool(name="psum", bufs=1))
         ctx.enter_context(tc.manual_schedule())
 
-        def sb(shape, dtype, name):
-            t = pool.tile(shape, dtype, name=name, tag=name, align_bytes=64)
-            return t
+        def sbuf(name, shape, dtype):
+            return pool.tile(shape, dtype, name=name, tag=name, align_bytes=64)
 
-        def load(src, g, c0, c1, name):
-            t = sb([P, PACK, c1 - c0], F32, name)
-            nc.sync.dma_start(out=t[:], in_=src[g * K_PASS : (g + 1) * K_PASS, c0:c1].rearrange("(p j) w -> p j w", j=PACK))
-            return t
-
-        x0 = [load(x, 0, a, b, "x0_" + str(a)) for a, b in ((0, 128), (128, 256), (256, 384), (384, 512))]
-        x1 = [load(x, 1, c, c + 256, "x1_" + str(c)) for c in range(0, 512, 256)]
-        wr = {}
-        for h in (0, 1):
-            for g in (0, 1):
-                wr[g, h] = load(w, g, 256 * h, 256 * h + 256, "w" + str(g) + str(h))
-        r_sb = sb([P, 4, T], F32, "r_sb")
-        nc.sync.dma_start(out=r_sb[:], in_=r.rearrange("(m p) t -> p m t", p=P))
-
-        xq = {(g, part): sb([P, T], U32, "xq" + str(g) + part) for g in (0, 1) for part in ("hi", "lo")}
-        xs = {(g, part): sb([P, T], U8, "xs" + str(g) + part) for g in (0, 1) for part in ("hi", "lo")}
-
-        def rows(ap):
+        def columns(ap):
             return ap.rearrange("p j (c i) -> p c j i", i=4)
 
-        def packed(ap):
+        def grouped(ap):
             return ap.rearrange("p (c i j) -> p c j i", i=4, j=PACK)
 
-        def unit(name, pieces, full):
-            n = sum(p[2] for p in pieces) * PACK
-            offs = [sum(p[2] for p in pieces[:i]) * PACK for i in range(len(pieces))]
-            return dict(name=name, pieces=pieces, n=n, offs=offs,
-                        top=None if full else sb([P, n], BF16, "top_" + name),
-                        hi32=sb([P, PACK, n // PACK], I32, "hi32_" + name) if full else None,
-                        hl=sb([P, 2 * n], BF16, "hl_" + name))
+        def load(name, src, g, c0, width):
+            raw = sbuf("raw_" + name, [P, PACK, width], F32)
+            rows = src[g * K_PASS : (g + 1) * K_PASS, c0 : c0 + width]
+            nc.sync.dma_start(out=raw[:], in_=rows.rearrange("(p j) c -> p j c", j=PACK))
+            size = width * PACK
+            hilo = sbuf("hilo_" + name, [P, 2 * size], BF16)
+            return dict(name=name, g=g, c0=c0, width=width, raw=raw, hilo=hilo, hi=hilo[:, 0:size], lo=hilo[:, size : 2 * size])
 
-        def trunc32(u, a, b):
-            raw, r0, width = u["pieces"][0]
-            nc.vector.tensor_scalar(out=u["hi32"][:, :, a:b], in0=raw[:, :, r0 + a : r0 + b].bitcast(I32), scalar1=MASK_ONE, scalar2=None, op0=AND)
+        x_codes = {}
+        x_scales = {}
+        for g in (0, 1):
+            for part in ("hi", "lo"):
+                x_codes[g, part] = sbuf("x_codes_%d%s" % (g, part), [P, T], U32)
+                x_scales[g, part] = sbuf("x_scales_%d%s" % (g, part), [P, T], U8)
 
-        def cast_hi(u):
-            nc.scalar.copy(out=packed(u["hl"][:, 0 : u["n"]]), in_=rows(u["hi32"][:].bitcast(F32)))
+        x0 = [load("x0_%d" % i, x, 0, P * i, P) for i in range(4)]
+        w0 = [load("w0_%d" % h, w, 0, HALF * h, HALF) for h in range(2)]
+        x1 = [load("x1_%d" % h, x, 1, HALF * h, HALF) for h in range(2)]
+        w1 = [load("w1_%d" % h, w, 1, HALF * h, HALF) for h in range(2)]
+        r_sb = sbuf("r", [P, ROW_TILES, T], F32)
+        nc.sync.dma_start(out=r_sb[:], in_=r.rearrange("(m p) t -> p m t", p=P))
 
-        def top_copy(u):
-            for (raw, r0, width), o in zip(u["pieces"], u["offs"]):
-                s = raw[:].bitcast(BF16)[:, :, 2 * r0 + 1 : 2 * (r0 + width) : 2]
-                nc.scalar.copy(out=packed(u["top"][:, o : o + width * PACK]), in_=rows(s))
+        for c in w0 + w1:
+            c["codes"] = sbuf("codes_" + c["name"], [P, 2 * HALF], U32)
+            c["scales"] = sbuf("scales_" + c["name"], [P, 2 * HALF], U8)
+        for c in x0[0:3]:
+            c["hi32"] = sbuf("hi32_" + c["name"], [P, PACK, c["width"]], I32)
+        for c in x0[3:] + w0 + x1 + w1:
+            c["top"] = sbuf("top_" + c["name"], [P, c["width"] * PACK], BF16)
 
-        def trunc(u):
-            nc.vector.tensor_scalar(out=u["hl"][:, 0 : u["n"]].bitcast(I32), in0=u["top"][:].bitcast(I32), scalar1=MASK_TWO, scalar2=None, op0=AND)
+        def truncate32(c, a, b):
+            nc.vector.tensor_scalar(out=c["hi32"][:, :, a:b], in0=c["raw"][:, :, a:b].bitcast(I32), scalar1=MASK_F32, scalar2=None, op0=ALU.bitwise_and)
 
-        def sub(u, i=0, a=0, b=None):
-            raw, r0, width = u["pieces"][i]
-            b = width if b is None else b
-            o = u["offs"][i]
-            if u["hi32"] is not None:
-                in1 = rows(u["hi32"][:, :, a:b].bitcast(F32))
+        def group32(c):
+            nc.scalar.copy(out=grouped(c["hi"]), in_=columns(c["hi32"][:].bitcast(F32)))
+
+        def group_top(c):
+            nc.scalar.copy(out=grouped(c["top"][:]), in_=columns(c["raw"][:].bitcast(BF16)[:, :, 1::2]))
+
+        def truncate(c):
+            nc.vector.tensor_scalar(out=c["hi"].bitcast(I32), in0=c["top"][:].bitcast(I32), scalar1=MASK_BF16_PAIR, scalar2=None, op0=ALU.bitwise_and)
+
+        def subtract(c, a, b):
+            if "hi32" in c:
+                hi = columns(c["hi32"][:, :, a:b].bitcast(F32))
             else:
-                in1 = packed(u["hl"][:, o + 4 * a : o + 4 * b])
-            nc.vector.tensor_tensor(out=packed(u["hl"][:, u["n"] + o + 4 * a : u["n"] + o + 4 * b]), in0=rows(raw[:, :, r0 + a : r0 + b]), in1=in1, op=SUB)
+                hi = grouped(c["hi"][:, PACK * a : PACK * b])
+            nc.vector.tensor_tensor(out=grouped(c["lo"][:, PACK * a : PACK * b]), in0=columns(c["raw"][:, :, a:b]), in1=hi, op=ALU.subtract)
 
-        def quant_x(u, g, c0, part):
-            n = u["n"]
-            s = slice(c0, c0 + n // 4)
-            src = u["hl"][:, 0:n] if part == "hi" else u["hl"][:, n : 2 * n]
-            nc.vector.quantize_mx(out=xq[g, part][:, s].bitcast(FP8X4), scales=xs[g, part][:, s], in_=src)
+        def quantize_x(c, part):
+            cols = slice(c["c0"], c["c0"] + c["width"])
+            key = c["g"], part
+            nc.vector.quantize_mx(out=x_codes[key][:, cols].bitcast(FP8X4), scales=x_scales[key][:, cols], in_=c[part])
 
-        wcodes = {}
+        def quantize_w(c, a, b):
+            nc.vector.quantize_mx(out=c["codes"][:, a:b].bitcast(FP8X4), scales=c["scales"][:, a:b], in_=c["hilo"][:, PACK * a : PACK * b])
 
-        def w_unit(name, keys):
-            u = unit(name, [(wr[g, m // 2], 128 * (m % 2), 128) for (g, m) in keys], False)
-            u["codes"] = sb([P, u["n"] // 2], U32, "wq_" + name)
-            u["scales"] = sb([P, u["n"] // 2], U8, "ws_" + name)
-            for i, (g, m) in enumerate(keys):
-                wcodes[g, m, "hi"] = (u, 128 * i)
-                wcodes[g, m, "lo"] = (u, u["n"] // 4 + 128 * i)
-            return u
+        acc = [psum.tile([P, T], F32, name="acc%d" % m) for m in range(ROW_TILES)]
 
-        def quant_w(u, a=0, b=4):
-            s = slice(a * P, b * P)
-            nc.vector.quantize_mx(out=u["codes"][:, s].bitcast(FP8X4), scales=u["scales"][:, s], in_=u["hl"][:, a * P * PACK : b * P * PACK])
+        def multiply(m, g, w_part, x_part, start=False, stop=False):
+            c = (w0, w1)[g][m // 2]
+            a = P * (m % 2) + (HALF if w_part == "lo" else 0)
+            nc.tensor.matmul_mx(
+                out=acc[m][:],
+                lhsT=c["codes"][:, a : a + P].bitcast(FP8X4),
+                lhsT_scale=c["scales"][:, a : a + P],
+                rhs=x_codes[g, x_part][:].bitcast(FP8X4),
+                rhs_scale=x_scales[g, x_part][:],
+                start=start,
+                stop=stop,
+            )
 
-        acc = [psum.tile([P, T], F32, name="acc" + str(m)) for m in range(4)]
+        def multiply_hi(h, g):
+            for m in (2 * h, 2 * h + 1):
+                multiply(m, g, "hi", "hi", start=(g == 0))
+                multiply(m, g, "hi", "lo")
 
-        def product(m, g, wpart, xpart, start, stop):
-            u, c = wcodes[g, m, wpart]
-            s = slice(c, c + P)
-            nc.tensor.matmul_mx(out=acc[m][:], lhsT=u["codes"][:, s].bitcast(FP8X4), lhsT_scale=u["scales"][:, s],
-                                rhs=xq[g, xpart][:].bitcast(FP8X4), rhs_scale=xs[g, xpart][:], start=start, stop=stop)
+        def multiply_lo(m, g):
+            multiply(m, g, "lo", "hi", stop=(g == 1))
 
-        def products(m, g):
-            product(m, g, "hi", "hi", g == 0, False)
-            product(m, g, "hi", "lo", False, False)
-            product(m, g, "lo", "hi", False, g == 1)
+        result = [sbuf("result%d" % m, [P, T], F32) for m in range(ROW_TILES)]
 
-        y = [sb([P, T], F32, "y" + str(m)) for m in range(4)]
+        def finish(m, a, b, store_from):
+            nc.vector.tensor_tensor(out=result[m][:, a:b], in0=acc[m][:, a:b], in1=r_sb[:, m, a:b], op=ALU.add)
+            if store_from is not None:
+                nc.sync.dma_start(out=out[P * m : P * (m + 1), store_from:b], in_=result[m][:, store_from:b])
 
-        def drain(m, a, b):
-            nc.vector.tensor_tensor(out=y[m][:, a:b], in0=acc[m][:, a:b], in1=r_sb[:, m, a:b], op=ADD)
-            nc.sync.dma_start(out=out[m * P : (m + 1) * P, a:b], in_=y[m][:, a:b])
+        truncate32(x0[0], 0, 64)
+        truncate32(x0[0], 64, 128)
+        group32(x0[0])
+        subtract(x0[0], 0, 64)
+        subtract(x0[0], 64, 128)
+        truncate32(x0[1], 0, 128)
+        group32(x0[1])
+        quantize_x(x0[0], "lo")
+        quantize_x(x0[0], "hi")
+        subtract(x0[1], 0, 128)
+        group_top(x0[3])
+        truncate32(x0[2], 0, 128)
+        group32(x0[2])
+        quantize_x(x0[1], "lo")
+        quantize_x(x0[1], "hi")
+        subtract(x0[2], 0, 128)
+        for c in w0 + x1 + w1:
+            group_top(c)
+        truncate(x0[3])
+        quantize_x(x0[2], "hi")
+        quantize_x(x0[2], "lo")
+        subtract(x0[3], 0, 128)
 
-        xa, xb, xc = [unit("x0u" + str(i), [(x0[i], 0, 128)], True) for i in (0, 1, 2)]
-        xd = unit("x0u3", [(x0[3], 0, 128)], False)
-        xe, xf = [unit("x1u" + str(i), [(x1[i], 0, 256)], False) for i in (0, 1)]
-        p0 = w_unit("p0", [(0, 0), (1, 0)])
-        p1 = w_unit("p1", [(0, 1), (1, 1)])
-        p2 = w_unit("p2", [(0, 2), (0, 3)])
-        p3 = w_unit("p3", [(1, 2), (1, 3)])
+        truncate(w0[0])
+        quantize_x(x0[3], "hi")
+        quantize_x(x0[3], "lo")
+        subtract(w0[0], 0, HALF)
+        quantize_w(w0[0], 0, HALF)
+        multiply_hi(0, 0)
+        truncate(w0[1])
+        quantize_w(w0[0], HALF, 2 * HALF)
+        multiply_lo(0, 0)
+        multiply_lo(1, 0)
+        subtract(w0[1], 0, HALF)
 
-        trunc32(xa, 0, 64)
-        trunc32(xa, 64, 128)
-        cast_hi(xa)
-        sub(xa, 0, 0, 64)
-        sub(xa, 0, 64, 128)
-        trunc32(xb, 0, 128)
-        cast_hi(xb)
-        top_copy(xd)
-        quant_x(xa, 0, 0, "lo")
-        quant_x(xa, 0, 0, "hi")
-        sub(xb)
-        trunc32(xc, 0, 128)
-        cast_hi(xc)
-        quant_x(xb, 0, 128, "lo")
-        quant_x(xb, 0, 128, "hi")
-        sub(xc)
-        prev = (xc, 0, 256)
-        for nxt in ((xd, 0, 384), (xe, 1, 0), (xf, 1, 256)):
-            if nxt[1] == 1:
-                top_copy(nxt[0])
-            trunc(nxt[0])
-            quant_x(*prev, "hi")
-            quant_x(*prev, "lo")
-            sub(nxt[0])
-            prev = nxt
-        top_copy(p0)
-        trunc(p0)
-        quant_x(*prev, "hi")
-        quant_x(*prev, "lo")
-        sub(p0, 0)
-        sub(p0, 1)
-        top_copy(p1)
-        trunc(p1)
-        top_copy(p2)
-        quant_w(p0)
-        products(0, 0)
-        products(0, 1)
-        sub(p1, 0)
-        sub(p1, 1)
-        trunc(p2)
-        top_copy(p3)
-        quant_w(p1)
-        products(1, 0)
-        products(1, 1)
-        sub(p2, 0)
-        trunc(p3)
-        sub(p2, 1)
-        quant_w(p3, 0, 2)
-        for m in (2, 3):
-            product(m, 1, "hi", "hi", True, False)
-            product(m, 1, "hi", "lo", False, False)
-        quant_w(p2)
-        product(2, 0, "hi", "hi", False, False)
-        product(2, 0, "hi", "lo", False, False)
-        product(2, 0, "lo", "hi", False, False)
-        product(3, 0, "hi", "hi", False, False)
-        drain(0, 0, T)
-        sub(p3, 0)
-        drain(1, 0, 256)
-        quant_w(p3, 2, 3)
-        product(2, 1, "lo", "hi", False, True)
-        product(3, 0, "hi", "lo", False, False)
-        product(3, 0, "lo", "hi", False, False)
-        sub(p3, 1)
-        drain(1, 256, T)
-        quant_w(p3, 3, 4)
-        product(3, 1, "lo", "hi", False, True)
-        drain(2, 0, T)
-        drain(3, 0, 256)
-        drain(3, 256, T)
+        truncate(x1[0])
+        quantize_w(w0[1], 0, HALF)
+        multiply_hi(1, 0)
+        subtract(x1[0], 0, HALF)
+        truncate(x1[1])
+        quantize_w(w0[1], HALF, 2 * HALF)
+        multiply_lo(2, 0)
+        multiply_lo(3, 0)
+        quantize_x(x1[0], "hi")
+        subtract(x1[1], 0, HALF)
+
+        truncate(w1[0])
+        quantize_x(x1[0], "lo")
+        quantize_x(x1[1], "hi")
+        quantize_x(x1[1], "lo")
+        quantize_w(w1[0], 0, HALF)
+        multiply_hi(0, 1)
+        subtract(w1[0], 0, HALF)
+        truncate(w1[1])
+        quantize_w(w1[0], HALF, 2 * HALF)
+        multiply_lo(0, 1)
+        multiply_lo(1, 1)
+        quantize_w(w1[1], 0, HALF)
+        multiply_hi(1, 1)
+        subtract(w1[1], 0, P)
+        finish(0, 0, T, 0)
+        quantize_w(w1[1], HALF, HALF + P)
+        multiply_lo(2, 1)
+        subtract(w1[1], P, HALF)
+        finish(1, 0, T // 2, None)
+        quantize_w(w1[1], HALF + P, 2 * HALF)
+        multiply_lo(3, 1)
+        finish(1, T // 2, T, 0)
+        finish(2, 0, T, 0)
+        finish(3, 0, T // 2, 0)
+        finish(3, T // 2, T, T // 2)

from contextlib import ExitStack

import concourse.mybir as mybir

K, N, T = 1024, 512, 512
FLOPS = 3 * 2 * K * N * T

F32 = mybir.dt.float32
BF16 = mybir.dt.bfloat16
I32 = mybir.dt.int32
U32 = mybir.dt.uint32
U8 = mybir.dt.uint8
FP8X4 = mybir.dt.float8_e4m3fn_x4
ALU = mybir.AluOpType

P = 128
PACK = 4
K_PASS = P * PACK
ROW_TILES = N // P
HALF = 256

MASK_F32 = -1048576
MASK_BF16_PAIR = -983056


def tile_mix_split3_fm_res_kernel(tc, w, x, r, out):
    nc = tc.nc
    with ExitStack() as ctx:
        pool = ctx.enter_context(tc.tile_pool(name="pool", bufs=1))
        psum = ctx.enter_context(tc.psum_pool(name="psum", bufs=1))
        ctx.enter_context(tc.manual_schedule())

        def sbuf(name, shape, dtype):
            return pool.tile(shape, dtype, name=name, tag=name, align_bytes=64)

        def columns(ap):
            return ap.rearrange("p j (c i) -> p c j i", i=4)

        def grouped(ap):
            return ap.rearrange("p (c i j) -> p c j i", i=4, j=PACK)

        def load(name, src, g, c0, width):
            raw = sbuf("raw_" + name, [P, PACK, width], F32)
            rows = src[g * K_PASS : (g + 1) * K_PASS, c0 : c0 + width]
            nc.sync.dma_start(out=raw[:], in_=rows.rearrange("(p j) c -> p j c", j=PACK))
            size = width * PACK
            hilo = sbuf("hilo_" + name, [P, 2 * size], BF16)
            return dict(name=name, g=g, c0=c0, width=width, raw=raw, hilo=hilo, hi=hilo[:, 0:size], lo=hilo[:, size : 2 * size])

        x_codes = {}
        x_scales = {}
        for g in (0, 1):
            for part in ("hi", "lo"):
                x_codes[g, part] = sbuf("x_codes_%d%s" % (g, part), [P, T], U32)
                x_scales[g, part] = sbuf("x_scales_%d%s" % (g, part), [P, T], U8)

        x0 = [load("x0_%d" % i, x, 0, P * i, P) for i in range(4)]
        w0 = [load("w0_%d" % h, w, 0, HALF * h, HALF) for h in range(2)]
        x1 = [load("x1_%d" % h, x, 1, HALF * h, HALF) for h in range(2)]
        w1 = [load("w1_%d" % h, w, 1, HALF * h, HALF) for h in range(2)]
        r_sb = sbuf("r", [P, ROW_TILES, T], F32)
        nc.sync.dma_start(out=r_sb[:], in_=r.rearrange("(m p) t -> p m t", p=P))

        for c in w0 + w1:
            c["codes"] = sbuf("codes_" + c["name"], [P, 2 * HALF], U32)
            c["scales"] = sbuf("scales_" + c["name"], [P, 2 * HALF], U8)
        for c in x0[0:3]:
            c["hi32"] = sbuf("hi32_" + c["name"], [P, PACK, c["width"]], I32)
        for c in x0[3:] + w0 + x1 + w1:
            c["top"] = sbuf("top_" + c["name"], [P, c["width"] * PACK], BF16)

        def truncate32(c, a, b):
            nc.vector.tensor_scalar(out=c["hi32"][:, :, a:b], in0=c["raw"][:, :, a:b].bitcast(I32), scalar1=MASK_F32, scalar2=None, op0=ALU.bitwise_and)

        def group32(c):
            nc.scalar.copy(out=grouped(c["hi"]), in_=columns(c["hi32"][:].bitcast(F32)))

        def group_top(c):
            nc.scalar.copy(out=grouped(c["top"][:]), in_=columns(c["raw"][:].bitcast(BF16)[:, :, 1::2]))

        def truncate(c):
            nc.vector.tensor_scalar(out=c["hi"].bitcast(I32), in0=c["top"][:].bitcast(I32), scalar1=MASK_BF16_PAIR, scalar2=None, op0=ALU.bitwise_and)

        def subtract(c, a, b):
            if "hi32" in c:
                hi = columns(c["hi32"][:, :, a:b].bitcast(F32))
            else:
                hi = grouped(c["hi"][:, PACK * a : PACK * b])
            nc.vector.tensor_tensor(out=grouped(c["lo"][:, PACK * a : PACK * b]), in0=columns(c["raw"][:, :, a:b]), in1=hi, op=ALU.subtract)

        def quantize_x(c, part):
            cols = slice(c["c0"], c["c0"] + c["width"])
            key = c["g"], part
            nc.vector.quantize_mx(out=x_codes[key][:, cols].bitcast(FP8X4), scales=x_scales[key][:, cols], in_=c[part])

        def quantize_w(c, a, b):
            nc.vector.quantize_mx(out=c["codes"][:, a:b].bitcast(FP8X4), scales=c["scales"][:, a:b], in_=c["hilo"][:, PACK * a : PACK * b])

        acc = [psum.tile([P, T], F32, name="acc%d" % m) for m in range(ROW_TILES)]

        def multiply(m, g, w_part, x_part, start=False, stop=False):
            c = (w0, w1)[g][m // 2]
            a = P * (m % 2) + (HALF if w_part == "lo" else 0)
            nc.tensor.matmul_mx(
                out=acc[m][:],
                lhsT=c["codes"][:, a : a + P].bitcast(FP8X4),
                lhsT_scale=c["scales"][:, a : a + P],
                rhs=x_codes[g, x_part][:].bitcast(FP8X4),
                rhs_scale=x_scales[g, x_part][:],
                start=start,
                stop=stop,
            )

        def multiply_hi(h, g):
            for m in (2 * h, 2 * h + 1):
                multiply(m, g, "hi", "hi", start=(g == 0))
                multiply(m, g, "hi", "lo")

        def multiply_lo(m, g):
            multiply(m, g, "lo", "hi", stop=(g == 1))

        result = [sbuf("result%d" % m, [P, T], F32) for m in range(ROW_TILES)]

        def finish(m, a, b, store_from):
            nc.vector.tensor_tensor(out=result[m][:, a:b], in0=acc[m][:, a:b], in1=r_sb[:, m, a:b], op=ALU.add)
            if store_from is not None:
                nc.sync.dma_start(out=out[P * m : P * (m + 1), store_from:b], in_=result[m][:, store_from:b])

        truncate32(x0[0], 0, 64)
        truncate32(x0[0], 64, 128)
        group32(x0[0])
        subtract(x0[0], 0, 64)
        subtract(x0[0], 64, 128)
        truncate32(x0[1], 0, 128)
        group32(x0[1])
        quantize_x(x0[0], "lo")
        quantize_x(x0[0], "hi")
        subtract(x0[1], 0, 128)
        group_top(x0[3])
        truncate32(x0[2], 0, 128)
        group32(x0[2])
        quantize_x(x0[1], "lo")
        quantize_x(x0[1], "hi")
        subtract(x0[2], 0, 128)
        for c in w0 + x1 + w1:
            group_top(c)
        truncate(x0[3])
        quantize_x(x0[2], "hi")
        quantize_x(x0[2], "lo")
        subtract(x0[3], 0, 128)

        truncate(w0[0])
        quantize_x(x0[3], "hi")
        quantize_x(x0[3], "lo")
        subtract(w0[0], 0, HALF)
        quantize_w(w0[0], 0, HALF)
        multiply_hi(0, 0)
        truncate(w0[1])
        quantize_w(w0[0], HALF, 2 * HALF)
        multiply_lo(0, 0)
        multiply_lo(1, 0)
        subtract(w0[1], 0, HALF)

        truncate(x1[0])
        quantize_w(w0[1], 0, HALF)
        multiply_hi(1, 0)
        subtract(x1[0], 0, HALF)
        truncate(x1[1])
        quantize_w(w0[1], HALF, 2 * HALF)
        multiply_lo(2, 0)
        multiply_lo(3, 0)
        quantize_x(x1[0], "hi")
        subtract(x1[1], 0, HALF)

        truncate(w1[0])
        quantize_x(x1[0], "lo")
        quantize_x(x1[1], "hi")
        quantize_x(x1[1], "lo")
        quantize_w(w1[0], 0, HALF)
        multiply_hi(0, 1)
        subtract(w1[0], 0, HALF)
        truncate(w1[1])
        quantize_w(w1[0], HALF, 2 * HALF)
        multiply_lo(0, 1)
        multiply_lo(1, 1)
        quantize_w(w1[1], 0, HALF)
        multiply_hi(1, 1)
        subtract(w1[1], 0, P)
        finish(0, 0, T, 0)
        quantize_w(w1[1], HALF, HALF + P)
        multiply_lo(2, 1)
        subtract(w1[1], P, HALF)
        finish(1, 0, T // 2, None)
        quantize_w(w1[1], HALF + P, 2 * HALF)
        multiply_lo(3, 1)
        finish(1, T // 2, T, 0)
        finish(2, 0, T, 0)
        finish(3, 0, T // 2, 0)
        finish(3, T // 2, T, T // 2)
